import numpy as np
import ml_dtypes


def mxq(x, axis, fmt="e4m3"):
    dtype, down = {"e4m3": (ml_dtypes.float8_e4m3fn, 7), "e5m2": (ml_dtypes.float8_e5m2, 14)}[fmt]
    v = np.moveaxis(np.asarray(x, np.float32).astype(ml_dtypes.bfloat16).astype(np.float64), axis, -1)
    blocks = v.reshape(v.shape[:-1] + (-1, 32))
    amax = np.abs(blocks).max(-1, keepdims=True)
    byte = np.maximum(np.where(amax > 0, np.frexp(amax)[1] - 1 + 127, 0) - down, 1)
    scale = np.exp2(byte - 127.0)
    codes = (blocks / scale).astype(np.float32).astype(dtype).astype(np.float64)
    return np.moveaxis((codes * scale).reshape(v.shape), -1, axis)


WIDE = False


def mx_kscale(k):
    if not WIDE:
        return np.ones(k)
    levels = np.array([10, -10, 5, -5, 0])
    if k % 512:
        return np.exp2(np.random.permutation(np.resize(levels, k // 32))).repeat(32)
    a = np.empty((k // 512, 16))
    for p in range(k // 512):
        a[p, :8] = np.random.permutation(np.resize(levels, 8))
        for g in range(8):
            far = levels[np.abs(levels - a[p, g]) >= 10]
            a[p, g + 8] = far[np.random.randint(len(far))]
    return np.exp2(a.ravel()).repeat(32)


def f64(x):
    return np.asarray(x).astype(np.float64)


def striped(idx):
    return np.tile(idx.reshape(-1, 16).T, (8, 1)).astype(np.uint16)


def unstriped(offs):
    return offs[:16].T.reshape(-1).astype(np.int64)


def striped8(idx):
    return np.concatenate([x.reshape(-1, 16).T for x in idx]).astype(np.uint16)


def runs(offs, k):
    lists = np.stack([offs[16 * r : 16 * r + 16].T.reshape(-1) for r in range(8)]).astype(np.int64)
    return lists[np.arange(k) % 512 // 64]


def pack_weight(w):
    k, n = w.shape
    w = f64(np.asarray(w, np.float32).astype(ml_dtypes.bfloat16)).reshape(k // 32, 32, n)
    amax = np.abs(w).max(1)
    byte = np.clip(np.where(amax > 0, np.frexp(amax)[1] - 1 + 127 - 7, 1), 1, 254)
    scaled = (w * np.exp2(127.0 - byte)[:, None, :]).reshape(k, n).astype(np.float32)
    words = np.ascontiguousarray(scaled.reshape(k // 512, 128, 4, n).transpose(0, 1, 3, 2)).astype(ml_dtypes.float8_e4m3fn).view(np.uint8)
    return words, np.ascontiguousarray(byte.astype(np.uint8).reshape(k // 512, 16, n))


def unpack_weight(words, scales):
    g, p, n, _ = words.shape
    vals = np.ascontiguousarray(words).view(ml_dtypes.float8_e4m3fn).astype(np.float64) * np.repeat(np.exp2(scales.astype(np.float64) - 127.0), 8, axis=1)[..., None]
    return vals.transpose(0, 1, 3, 2).reshape(g * 512, n)


def sigmoid(v):
    return 1.0 / (1.0 + np.exp(-np.maximum(v, -700.0)))


K, T, S, G, H = 512, 1024, 512, 2048, 512


def setup_inputs():
    n = np.random.standard_normal
    s = mx_kscale(K)[:, None]
    packed_xT = pack_weight(n((K, T)) * s)
    packed_dT = pack_weight(n((K, G)) / s)
    return {
        "x_words": packed_xT[0],
        "x_scales": packed_xT[1],
        "d_words": packed_dT[0],
        "d_scales": packed_dT[1],
        "gs": (np.random.uniform(0.5, 1.5, (K, 1)) * s).astype(np.float32),
        "sl": np.random.uniform(1.5, 3.0, (H, 1)).astype(np.float32),
        "th": (0.5 * n((H, 1))).astype(np.float32),
        "offs": striped(np.random.permutation(T)[:S]),
        "k1": striped8(np.random.randint(0, G, (8, H))),
        "n1": striped(np.random.permutation(S)),
        "n2": striped(np.random.permutation(S)),
        "k2": striped8(np.random.randint(0, G, (8, H))),
        "n3": striped8(np.stack([np.random.permutation(S) for _ in range(8)])),
        "n4": striped8(np.stack([np.random.permutation(S) for _ in range(8)])),
    }


def reference(x_words, x_scales, d_words, d_scales, gs, sl, th, offs, k1, n1, n2, k2, n3, n4):
    d_k2 = unpack_weight(d_words, d_scales)[np.arange(K)[:, None], runs(k2, K)]
    d_k1 = unpack_weight(d_words, d_scales)[np.arange(K)[:, None], runs(k1, K)]
    xq = unpack_weight(x_words, x_scales)[:, unstriped(offs)]
    h = 0.0625 * (d_k1.T @ xq)
    sm = np.maximum(h, h[:, unstriped(n2)])
    ds = np.zeros((H, S))
    ds[:, unstriped(n1)] = sm
    z = f64(gs) * (ds * sigmoid(h))
    h2 = 0.0625 * ((d_k2.T @ mxq(z, 0, "e4m3")))
    sg = sigmoid(f64(sl) * (h2[np.arange(H)[:, None], runs(n3, H)] - f64(th)))
    return 1.5 * (h2 * (sg - (sg[np.arange(H)[:, None], runs(n4, H)])))

@@ -1,0 +1,221 @@
+from contextlib import ExitStack
+
+import concourse.mybir as mybir
+
+K, T, S, G, H = 512, 1024, 512, 2048, 512
+FLOPS = 2 * 2 * K * H * S
+
+F32 = mybir.dt.float32
+BF16 = mybir.dt.bfloat16
+I32 = mybir.dt.int32
+U32 = mybir.dt.uint32
+U16 = mybir.dt.uint16
+U8 = mybir.dt.uint8
+FP8X4 = mybir.dt.float8_e4m3fn_x4
+ALU = mybir.AluOpType
+ACT = mybir.ActivationFunctionType
+
+P = 128
+PACK = 4
+HALF = S // 2
+SPLIT = 192
+
+
+def entries(offsets, start, stop):
+    return offsets[:, start // 16 : stop // 16]
+
+
+def tile_picked_codesendgedb_none_p_kernel(
+    tc, x_words, x_scales, d_words, d_scales, gs, sl, th, offs, k1, n1, n2, k2, n3, n4, out
+):
+    nc = tc.nc
+    halves = [(0, HALF), (HALF, S)]
+    with ExitStack() as ctx:
+        keep = ctx.enter_context(tc.tile_pool(name="keep", bufs=1))
+        psum = ctx.enter_context(tc.psum_pool(name="psum", bufs=1))
+
+        def load_list(name, source):
+            offsets = keep.tile([P, S // 16], U16, name=name)
+            nc.sync.dma_start(offsets[:], source)
+            return offsets
+
+        def row_tile(name, tag=None):
+            return keep.tile([P, S], F32, name=name, tag=tag or name, align_bytes=64)
+
+        d_bytes = keep.tile([P, G], U8, name="d_bytes", align_bytes=64)
+        x_bytes = keep.tile([P, T], U8, name="x_bytes", align_bytes=64)
+        planes = [keep.tile([P, width], U8, name="plane%d" % i, align_bytes=64) for i, width in enumerate((H + S, H))]
+        nc.vector.memset(d_bytes[:].bitcast(I32), 0)
+        nc.vector.memset(x_bytes[:].bitcast(I32), 0)
+        for plane in planes:
+            nc.vector.memset(plane[:].bitcast(I32), 0)
+
+        k1_list = load_list("k1_list", k1)
+        offs_list = load_list("offs_list", offs)
+        k2_list = load_list("k2_list", k2)
+        nc.scalar.dma_start(d_bytes[0:P:8, :].bitcast(I32), d_scales[0].bitcast(I32))
+        nc.scalar.dma_start(x_bytes[0:P:8, :].bitcast(I32), x_scales[0].bitcast(I32))
+        x_table = keep.tile([P, T], I32, name="x_table", align_bytes=64)
+        nc.sync.dma_start(x_table[:], x_words[0].rearrange("p c r -> p (c r)").bitcast(I32))
+        d_table = keep.tile([P, G], I32, name="d_table", align_bytes=64)
+        nc.sync.dma_start(d_table[:], d_words[0].rearrange("p c r -> p (c r)").bitcast(I32))
+        n2_list = load_list("n2_list", n2)
+        n1_list = load_list("n1_list", n1)
+        n3_list = load_list("n3_list", n3)
+        n4_list = load_list("n4_list", n4)
+        gain = keep.tile([P, PACK], F32, name="gain")
+        slope = keep.tile([P, PACK], F32, name="slope")
+        threshold = keep.tile([P, PACK], F32, name="threshold")
+        for column, source in ((gain, gs), (slope, sl), (threshold, th)):
+            nc.gpsimd.dma_start(column[:], source.rearrange("(p t) o -> p (t o)", t=PACK))
+
+        def deal_bytes(picked, dealt):
+            nc.vector.tensor_copy(
+                dealt[:, 0:H].rearrange("p (t m) -> p m t", t=PACK), picked[:].rearrange("p (m t) -> p m t", t=PACK)
+            )
+
+        def place_bytes(dealt, plane):
+            for q in range(4):
+                nc.sync.dma_start(plane[32 * q : 32 * q + 4, :].bitcast(I32), dealt[32 * q : 32 * q + 32 : 8, :].bitcast(I32))
+
+        def deal_words(picked, dealt, start, stop):
+            nc.vector.tensor_copy(
+                dealt[:].rearrange("p (t m) -> p m t", t=PACK)[:, start // PACK : stop // PACK, :],
+                picked[:].rearrange("p (m t) -> p m t", t=PACK),
+            )
+
+        picked_bytes1 = keep.tile([P, H], U8, name="picked_bytes1", align_bytes=64)
+        nc.vector.tensor_copy(picked_bytes1[:], d_bytes[:].indirect(k1_list[:]))
+        xq_bytes = keep.tile([P, S], U8, name="xq_bytes", align_bytes=64)
+        nc.vector.tensor_copy(xq_bytes[:], x_bytes[:].indirect(offs_list[:]))
+        dealt_bytes1 = keep.tile([P, H + S], U8, name="dealt_bytes1", align_bytes=64)
+        deal_bytes(picked_bytes1, dealt_bytes1)
+        nc.vector.tensor_copy(dealt_bytes1[:, H:].bitcast(I32), xq_bytes[:].bitcast(I32))
+        place_bytes(dealt_bytes1, planes[0])
+        xq_words = keep.tile([P, S], U32, name="xq_words", align_bytes=64)
+        nc.vector.tensor_copy(xq_words[:], x_table[:].bitcast(U32).indirect(offs_list[:]))
+        w1 = keep.tile([P, H], U32, name="w1", align_bytes=64)
+        picked1 = [keep.tile([P, HALF], U32, name="picked1_%d" % i, tag="picked%d" % i, align_bytes=64) for i in range(2)]
+        for picked, (a, b) in zip(picked1, halves):
+            nc.vector.tensor_copy(picked[:], d_table[:].bitcast(U32).indirect(entries(k1_list, a, b)))
+        for picked, (a, b) in zip(picked1, halves):
+            deal_words(picked, w1, a, b)
+
+        h_banks = [psum.tile([P, S], F32, name="h_bank%d" % t) for t in range(PACK)]
+        for t in range(PACK):
+            columns = slice(P * t, P * (t + 1))
+            nc.tensor.matmul_mx(
+                h_banks[t][:], lhsT=w1[:, columns].bitcast(FP8X4), lhsT_scale=planes[0][:, columns],
+                rhs=xq_words[:].bitcast(FP8X4), rhs_scale=planes[0][:, H:], start=True, stop=True,
+            )
+
+        picked_bytes2 = keep.tile([P, H], U8, name="picked_bytes2", tag="picked0", align_bytes=64)
+        picked2 = keep.tile([P, H], U32, name="picked2", tag="picked1", align_bytes=64)
+        w2 = keep.tile([P, H], U32, name="w2", align_bytes=64)
+        nc.vector.tensor_copy(picked_bytes2[:], d_bytes[:].indirect(k2_list[:]))
+        nc.vector.tensor_copy(picked2[:], d_table[:].bitcast(U32).indirect(k2_list[:]))
+        dealt_bytes2 = keep.tile([P, H], U8, name="dealt_bytes2", align_bytes=64)
+        deal_bytes(picked_bytes2, dealt_bytes2)
+        place_bytes(dealt_bytes2, planes[1])
+        deal_words(picked2, w2, 0, H)
+        bias = keep.tile([P, PACK], F32, name="bias")
+        nc.vector.scalar_tensor_tensor(bias[:], slope[:], -1.0, threshold[:], ALU.mult, ALU.mult)
+
+        gates = [row_tile("gate%d" % t) for t in range(PACK)]
+        h = [row_tile("h%d" % t) for t in range(PACK)]
+        fetched = [row_tile("fetched%d" % t) for t in range(PACK)]
+        larger = [row_tile("larger%d" % t) for t in range(PACK)]
+
+        def gate(t):
+            nc.scalar.activation(gates[t][:], h_banks[t][:], ACT.Sigmoid, scale=0.0625)
+
+        def take_larger(t):
+            nc.vector.tensor_tensor(larger[t][:], h[t][:], fetched[t][:], ALU.max)
+
+        def send(engine, window, t, a, b):
+            target = window[:].indirect(entries(n1_list, a, b))
+            if engine == "vector":
+                nc.vector.tensor_copy(target, larger[t][:, a:b])
+            else:
+                nc.scalar.activation(target, larger[t][:, a:b], ACT.Copy)
+
+        z_rows = keep.tile([P, PACK, S], BF16, name="z_rows", align_bytes=64)
+
+        def weigh(t, window):
+            nc.vector.scalar_tensor_tensor(z_rows[:, t, :], window[:], gain[:, t : t + 1], gates[t][:], ALU.mult, ALU.mult)
+
+        gate(0)
+        for t in range(PACK):
+            nc.scalar.activation(h[t][:], h_banks[t][:], ACT.Copy, scale=0.0625)
+            for a, b in halves:
+                nc.scalar.activation(fetched[t][:, a:b], h[t][:].indirect(entries(n2_list, a, b)), ACT.Copy)
+        for t in range(1, PACK):
+            gate(t)
+
+        take_larger(0)
+        sent0 = row_tile("sent0")
+        for a, b in halves:
+            send("vector", sent0, 0, a, b)
+        weigh(0, sent0)
+        for t in range(1, PACK):
+            take_larger(t)
+        sent3 = row_tile("sent3")
+        for a, b in halves:
+            send("scalar", sent3, 3, a, b)
+        sent2 = row_tile("sent2", tag="h3")
+        send("vector", sent2, 2, 0, SPLIT)
+        sent1 = row_tile("sent1", tag="fetched3")
+        for a, b in halves:
+            send("vector", sent1, 1, a, b)
+        send("scalar", sent2, 2, SPLIT, S)
+        weigh(1, sent1)
+        weigh(3, sent3)
+        weigh(2, sent2)
+
+        z_grouped = keep.tile([P, S, PACK], BF16, name="z_grouped", align_bytes=64)
+        nc.vector.tensor_copy(
+            z_grouped[:].rearrange("p (c i) t -> p c t i", i=4), z_rows[:].rearrange("p t (c i) -> p c t i", i=4)
+        )
+        z_words = keep.tile([P, S], U32, name="z_words", align_bytes=64)
+        z_bytes = keep.tile([P, S], U8, name="z_bytes", align_bytes=64)
+        nc.vector.quantize_mx(z_words[:].bitcast(FP8X4), z_bytes[:], z_grouped[:].rearrange("p s t -> p (s t)"))
+
+        h2_banks = [psum.tile([P, S], F32, name="h2_bank%d" % t) for t in range(PACK)]
+        for t in range(PACK):
+            columns = slice(P * t, P * (t + 1))
+            nc.tensor.matmul_mx(
+                h2_banks[t][:], lhsT=w2[:, columns].bitcast(FP8X4), lhsT_scale=planes[1][:, columns],
+                rhs=z_words[:].bitcast(FP8X4), rhs_scale=z_bytes[:], start=True, stop=True,
+            )
+
+        h2 = [row_tile("h2_%d" % t) for t in range(PACK)]
+        sg = [row_tile("sg%d" % t) for t in range(PACK)]
+        other = [row_tile("other%d" % t) for t in range(PACK)]
+        difference = [row_tile("difference%d" % t) for t in range(PACK)]
+        result = [row_tile("result%d" % t) for t in range(PACK)]
+        out_rows = out.rearrange("(p t) s -> p t s", t=PACK)
+
+        nc.scalar.activation(h2[0][:], h2_banks[0][:], ACT.Copy, scale=0.0625)
+        for t in range(1, PACK):
+            nc.vector.tensor_scalar(h2[t][:], h2_banks[t][:], 0.0625, None, ALU.mult)
+        for t in range(PACK):
+            for a, b in halves:
+                nc.scalar.activation(
+                    sg[t][:, a:b], h2[t][:].indirect(entries(n3_list, a, b)), ACT.Sigmoid,
+                    bias=bias[:, t : t + 1], scale=slope[:, t : t + 1],
+                )
+        for t in range(2):
+            nc.vector.tensor_copy(other[t][:], sg[t][:])
+            for a, b in halves:
+                nc.vector.tensor_tensor(
+                    difference[t][:, a:b], sg[t][:].indirect(entries(n4_list, a, b)), other[t][:, a:b], ALU.subtract
+                )
+            nc.vector.scalar_tensor_tensor(result[t][:], difference[t][:], -1.5, h2[t][:], ALU.mult, ALU.mult)
+            nc.sync.dma_start(out_rows[:, t, :], result[t][:])
+        for t in range(2, PACK):
+            for a, b in halves:
+                nc.scalar.activation(other[t][:, a:b], sg[t][:].indirect(entries(n4_list, a, b)), ACT.Copy)
+            for a, b in halves:
+                nc.vector.tensor_tensor(difference[t][:, a:b], other[t][:, a:b], sg[t][:, a:b], ALU.subtract)
+                nc.vector.scalar_tensor_tensor(result[t][:, a:b], difference[t][:, a:b], -1.5, h2[t][:, a:b], ALU.mult, ALU.mult)
+                nc.sync.dma_start(out_rows[:, t, a:b], result[t][:, a:b])

@@ -18,7 +18,9 @@ ACT = mybir.ActivationFunctionType
 P = 128
 PACK = 4
 HALF = S // 2
-SPLIT = 192
+SPLIT = 320
+WIDE = 704
+FIRST = 32
 
 
 def entries(offsets, start, stop):
@@ -52,14 +54,14 @@ def tile_picked_codesendgedb_none_p_kernel(
 
         k1_list = load_list("k1_list", k1)
         offs_list = load_list("offs_list", offs)
-        k2_list = load_list("k2_list", k2)
-        nc.scalar.dma_start(d_bytes[0:P:8, :].bitcast(I32), d_scales[0].bitcast(I32))
-        nc.scalar.dma_start(x_bytes[0:P:8, :].bitcast(I32), x_scales[0].bitcast(I32))
+        nc.sync.dma_start(d_bytes[0:P:8, :].bitcast(I32), d_scales[0].bitcast(I32))
+        nc.sync.dma_start(x_bytes[0:P:8, :].bitcast(I32), x_scales[0].bitcast(I32))
         x_table = keep.tile([P, T], I32, name="x_table", align_bytes=64)
         nc.sync.dma_start(x_table[:], x_words[0].rearrange("p c r -> p (c r)").bitcast(I32))
+        k2_list = load_list("k2_list", k2)
+        n2_list = load_list("n2_list", n2)
         d_table = keep.tile([P, G], I32, name="d_table", align_bytes=64)
         nc.sync.dma_start(d_table[:], d_words[0].rearrange("p c r -> p (c r)").bitcast(I32))
-        n2_list = load_list("n2_list", n2)
         n1_list = load_list("n1_list", n1)
         n3_list = load_list("n3_list", n3)
         n4_list = load_list("n4_list", n4)
@@ -69,14 +71,19 @@ def tile_picked_codesendgedb_none_p_kernel(
         for column, source in ((gain, gs), (slope, sl), (threshold, th)):
             nc.gpsimd.dma_start(column[:], source.rearrange("(p t) o -> p (t o)", t=PACK))
 
+        product = keep.tile([P, PACK], F32, name="product")
+        bias = keep.tile([P, PACK], F32, name="bias")
+        nc.gpsimd.tensor_tensor(product[:], slope[:], threshold[:], ALU.mult)
+        nc.gpsimd.tensor_scalar(bias[:], product[:], -1.0, 0.0, ALU.mult, ALU.add)
+
         def deal_bytes(picked, dealt):
             nc.vector.tensor_copy(
                 dealt[:, 0:H].rearrange("p (t m) -> p m t", t=PACK), picked[:].rearrange("p (m t) -> p m t", t=PACK)
             )
 
-        def place_bytes(dealt, plane):
+        def place_bytes(dealt, plane, queues):
             for q in range(4):
-                nc.sync.dma_start(plane[32 * q : 32 * q + 4, :].bitcast(I32), dealt[32 * q : 32 * q + 32 : 8, :].bitcast(I32))
+                queues[q % len(queues)].dma_start(plane[32 * q : 32 * q + 4, :].bitcast(I32), dealt[32 * q : 32 * q + 32 : 8, :].bitcast(I32))
 
         def deal_words(picked, dealt, start, stop):
             nc.vector.tensor_copy(
@@ -91,7 +98,7 @@ def tile_picked_codesendgedb_none_p_kernel(
         dealt_bytes1 = keep.tile([P, H + S], U8, name="dealt_bytes1", align_bytes=64)
         deal_bytes(picked_bytes1, dealt_bytes1)
         nc.vector.tensor_copy(dealt_bytes1[:, H:].bitcast(I32), xq_bytes[:].bitcast(I32))
-        place_bytes(dealt_bytes1, planes[0])
+        place_bytes(dealt_bytes1, planes[0], [nc.sync, nc.scalar])
         xq_words = keep.tile([P, S], U32, name="xq_words", align_bytes=64)
         nc.vector.tensor_copy(xq_words[:], x_table[:].bitcast(U32).indirect(offs_list[:]))
         w1 = keep.tile([P, H], U32, name="w1", align_bytes=64)
@@ -116,21 +123,20 @@ def tile_picked_codesendgedb_none_p_kernel(
         nc.vector.tensor_copy(picked2[:], d_table[:].bitcast(U32).indirect(k2_list[:]))
         dealt_bytes2 = keep.tile([P, H], U8, name="dealt_bytes2", align_bytes=64)
         deal_bytes(picked_bytes2, dealt_bytes2)
-        place_bytes(dealt_bytes2, planes[1])
+        place_bytes(dealt_bytes2, planes[1], [nc.sync])
         deal_words(picked2, w2, 0, H)
-        bias = keep.tile([P, PACK], F32, name="bias")
-        nc.vector.scalar_tensor_tensor(bias[:], slope[:], -1.0, threshold[:], ALU.mult, ALU.mult)
 
         gates = [row_tile("gate%d" % t) for t in range(PACK)]
-        h = [row_tile("h%d" % t) for t in range(PACK)]
+        h = [keep.tile([P, WIDE], F32, name="h%d" % t, align_bytes=64) for t in range(PACK)]
         fetched = [row_tile("fetched%d" % t) for t in range(PACK)]
-        larger = [row_tile("larger%d" % t) for t in range(PACK)]
+        larger = {}
 
-        def gate(t):
-            nc.scalar.activation(gates[t][:], h_banks[t][:], ACT.Sigmoid, scale=0.0625)
+        def gate(t, a, b):
+            nc.scalar.activation(gates[t][:, a:b], h_banks[t][:, a:b], ACT.Sigmoid, scale=0.0625)
 
-        def take_larger(t):
-            nc.vector.tensor_tensor(larger[t][:], h[t][:], fetched[t][:], ALU.max)
+        def take_larger(t, tag=None):
+            larger[t] = row_tile("larger%d" % t, tag)
+            nc.vector.scalar_tensor_tensor(larger[t][:], h_banks[t][:], 0.0625, fetched[t][:], ALU.mult, ALU.max)
 
         def send(engine, window, t, a, b):
             target = window[:].indirect(entries(n1_list, a, b))
@@ -141,44 +147,55 @@ def tile_picked_codesendgedb_none_p_kernel(
 
         z_rows = keep.tile([P, PACK, S], BF16, name="z_rows", align_bytes=64)
 
-        def weigh(t, window):
-            nc.vector.scalar_tensor_tensor(z_rows[:, t, :], window[:], gain[:, t : t + 1], gates[t][:], ALU.mult, ALU.mult)
+        def weigh(t, window, a, b):
+            nc.vector.scalar_tensor_tensor(z_rows[:, t, a:b], window[:, a:b], gain[:, t : t + 1], gates[t][:, a:b], ALU.mult, ALU.mult)
 
-        gate(0)
+        gate(0, 0, FIRST)
         for t in range(PACK):
-            nc.scalar.activation(h[t][:], h_banks[t][:], ACT.Copy, scale=0.0625)
-            for a, b in halves:
-                nc.scalar.activation(fetched[t][:, a:b], h[t][:].indirect(entries(n2_list, a, b)), ACT.Copy)
-        for t in range(1, PACK):
-            gate(t)
+            nc.scalar.activation(h[t][:, 0:S], h_banks[t][:], ACT.Copy, scale=0.0625)
+            nc.scalar.activation(fetched[t][:], h[t][:].indirect(n2_list[:]), ACT.Copy)
 
         take_larger(0)
-        sent0 = row_tile("sent0")
-        for a, b in halves:
-            send("vector", sent0, 0, a, b)
-        weigh(0, sent0)
-        for t in range(1, PACK):
-            take_larger(t)
-        sent3 = row_tile("sent3")
-        for a, b in halves:
-            send("scalar", sent3, 3, a, b)
-        sent2 = row_tile("sent2", tag="h3")
-        send("vector", sent2, 2, 0, SPLIT)
-        sent1 = row_tile("sent1", tag="fetched3")
-        for a, b in halves:
-            send("vector", sent1, 1, a, b)
-        send("scalar", sent2, 2, SPLIT, S)
-        weigh(1, sent1)
-        weigh(3, sent3)
-        weigh(2, sent2)
+        sent0 = keep.tile([P, WIDE], F32, name="sent0", align_bytes=64)
+        send("vector", sent0, 0, 0, S)
+        take_larger(1, "larger0")
+        take_larger(2)
+        take_larger(3)
+        sent3 = keep.tile([P, WIDE], F32, name="sent3", align_bytes=64)
+        send("vector", sent3, 3, 0, S)
+        sent1 = row_tile("sent1", tag="h3")
+        send("scalar", sent1, 1, 0, HALF)
+        sent2 = row_tile("sent2", tag="fetched3")
+        send("scalar", sent2, 2, 0, SPLIT)
+        send("vector", sent2, 2, SPLIT, S)
+        for t in (0, 3, 2, 1):
+            gate(t, FIRST if t == 0 else 0, S)
+        send("scalar", sent1, 1, HALF, S)
+        weigh(0, sent0, 0, S)
+        weigh(3, sent3, 0, S)
+        weigh(2, sent2, 0, S)
 
         z_grouped = keep.tile([P, S, PACK], BF16, name="z_grouped", align_bytes=64)
-        nc.vector.tensor_copy(
-            z_grouped[:].rearrange("p (c i) t -> p c t i", i=4), z_rows[:].rearrange("p t (c i) -> p c t i", i=4)
-        )
         z_words = keep.tile([P, S], U32, name="z_words", align_bytes=64)
         z_bytes = keep.tile([P, S], U8, name="z_bytes", align_bytes=64)
-        nc.vector.quantize_mx(z_words[:].bitcast(FP8X4), z_bytes[:], z_grouped[:].rearrange("p s t -> p (s t)"))
+
+        def group(copy, a, b):
+            copy(
+                z_grouped[:, a:b, :].rearrange("p (c i) t -> p c t i", i=4),
+                z_rows[:, :, a:b].rearrange("p t (c i) -> p c t i", i=4),
+            )
+
+        def quantise(a, b):
+            nc.vector.quantize_mx(z_words[:, a:b].bitcast(FP8X4), z_bytes[:, a:b], z_grouped[:, a:b, :].rearrange("p s t -> p (s t)"))
+
+        weigh(1, sent1, 0, P)
+        weigh(1, sent1, HALF, S)
+        weigh(1, sent1, P, HALF)
+        group(nc.scalar.copy, 0, P)
+        group(nc.vector.tensor_copy, HALF, S)
+        group(nc.vector.tensor_copy, P, HALF)
+        quantise(HALF, S)
+        quantise(0, HALF)
 
         h2_banks = [psum.tile([P, S], F32, name="h2_bank%d" % t) for t in range(PACK)]
         for t in range(PACK):
@@ -188,34 +205,51 @@ def tile_picked_codesendgedb_none_p_kernel(
                 rhs=z_words[:].bitcast(FP8X4), rhs_scale=z_bytes[:], start=True, stop=True,
             )
 
-        h2 = [row_tile("h2_%d" % t) for t in range(PACK)]
-        sg = [row_tile("sg%d" % t) for t in range(PACK)]
+        h2 = [keep.tile([P, 2 * S], F32, name="h2_%d" % t, align_bytes=64) for t in range(PACK)]
+        sg = [keep.tile([P, 2 * S], F32, name="sg%d" % t, align_bytes=64) for t in range(PACK)]
         other = [row_tile("other%d" % t) for t in range(PACK)]
         difference = [row_tile("difference%d" % t) for t in range(PACK)]
         result = [row_tile("result%d" % t) for t in range(PACK)]
         out_rows = out.rearrange("(p t) s -> p t s", t=PACK)
 
-        nc.scalar.activation(h2[0][:], h2_banks[0][:], ACT.Copy, scale=0.0625)
-        for t in range(1, PACK):
-            nc.vector.tensor_scalar(h2[t][:], h2_banks[t][:], 0.0625, None, ALU.mult)
-        for t in range(PACK):
-            for a, b in halves:
+        def leave_bank(t):
+            nc.vector.tensor_scalar(h2[t][:, 0:S], h2_banks[t][:], 0.0625, None, ALU.mult)
+
+        def fetch_sg(t, pieces):
+            for a, b in pieces:
                 nc.scalar.activation(
                     sg[t][:, a:b], h2[t][:].indirect(entries(n3_list, a, b)), ACT.Sigmoid,
                     bias=bias[:, t : t + 1], scale=slope[:, t : t + 1],
                 )
+
+        def duplicate(t, pieces):
+            for a, b in pieces:
+                nc.vector.tensor_copy(other[t][:, a:b], sg[t][:, a:b])
+
+        def finish(t, a, b):
+            nc.vector.scalar_tensor_tensor(result[t][:, a:b], difference[t][:, a:b], -1.5, h2[t][:, a:b], ALU.mult, ALU.mult)
+            nc.sync.dma_start(out_rows[:, t, a:b], result[t][:, a:b])
+
+        nc.scalar.activation(h2[0][:, 0:S], h2_banks[0][:], ACT.Copy, scale=0.0625)
+        leave_bank(1)
+        leave_bank(2)
+        fetch_sg(0, halves)
+        duplicate(0, halves)
+        leave_bank(3)
+        for t in range(1, PACK):
+            fetch_sg(t, [(0, S)])
         for t in range(2):
-            nc.vector.tensor_copy(other[t][:], sg[t][:])
-            for a, b in halves:
+            if t > 0:
+                duplicate(t, [(0, S)])
+            for a, b in halves if t == 0 else [(0, S)]:
                 nc.vector.tensor_tensor(
                     difference[t][:, a:b], sg[t][:].indirect(entries(n4_list, a, b)), other[t][:, a:b], ALU.subtract
                 )
-            nc.vector.scalar_tensor_tensor(result[t][:], difference[t][:], -1.5, h2[t][:], ALU.mult, ALU.mult)
-            nc.sync.dma_start(out_rows[:, t, :], result[t][:])
+            finish(t, 0, S)
         for t in range(2, PACK):
             for a, b in halves:
                 nc.scalar.activation(other[t][:, a:b], sg[t][:].indirect(entries(n4_list, a, b)), ACT.Copy)
             for a, b in halves:
                 nc.vector.tensor_tensor(difference[t][:, a:b], other[t][:, a:b], sg[t][:, a:b], ALU.subtract)
-                nc.vector.scalar_tensor_tensor(result[t][:, a:b], difference[t][:, a:b], -1.5, h2[t][:, a:b], ALU.mult, ALU.mult)
-                nc.sync.dma_start(out_rows[:, t, a:b], result[t][:, a:b])
+            for a, b in halves:
+                finish(t, a, b)

@@ -69,7 +69,7 @@ def tile_picked_codesendgedb_none_p_kernel(
         slope = keep.tile([P, PACK], F32, name="slope")
         threshold = keep.tile([P, PACK], F32, name="threshold")
         for column, source in ((gain, gs), (slope, sl), (threshold, th)):
-            nc.gpsimd.dma_start(column[:], source.rearrange("(p t) o -> p (t o)", t=PACK))
+            nc.scalar.dma_start(column[:], source.rearrange("(p t) o -> p (t o)", t=PACK))
 
         product = keep.tile([P, PACK], F32, name="product")
         bias = keep.tile([P, PACK], F32, name="bias")
@@ -78,7 +78,7 @@ def tile_picked_codesendgedb_none_p_kernel(
 
         def deal_bytes(picked, dealt):
             nc.vector.tensor_copy(
-                dealt[:, 0:H].rearrange("p (t m) -> p m t", t=PACK), picked[:].rearrange("p (m t) -> p m t", t=PACK)
+                dealt[:, 0:H].rearrange("p (t m) -> p t m", t=PACK), picked[:].rearrange("p (m t) -> p t m", t=PACK)
             )
 
         def place_bytes(dealt, plane, queues):
@@ -197,18 +197,26 @@ def tile_picked_codesendgedb_none_p_kernel(
         quantise(HALF, S)
         quantise(0, HALF)
 
-        h2_banks = [psum.tile([P, S], F32, name="h2_bank%d" % t) for t in range(PACK)]
-        for t in range(PACK):
+        def second_product(bank, t, a, b):
             columns = slice(P * t, P * (t + 1))
             nc.tensor.matmul_mx(
-                h2_banks[t][:], lhsT=w2[:, columns].bitcast(FP8X4), lhsT_scale=planes[1][:, columns],
-                rhs=z_words[:].bitcast(FP8X4), rhs_scale=z_bytes[:], start=True, stop=True,
+                bank[:], lhsT=w2[:, columns].bitcast(FP8X4), lhsT_scale=planes[1][:, columns],
+                rhs=z_words[:, a:b].bitcast(FP8X4), rhs_scale=z_bytes[:, a:b], start=True, stop=True,
             )
+
+        h2_late = psum.tile([P, HALF], F32, name="h2_late")
+        h2_early = psum.tile([P, HALF], F32, name="h2_early", tag="h_bank0")
+        second_product(h2_early, 0, HALF, S)
+        second_product(h2_late, 0, 0, HALF)
+        h2_banks = {}
+        for t in range(1, PACK):
+            h2_banks[t] = psum.tile([P, S], F32, name="h2_bank%d" % t)
+            second_product(h2_banks[t], t, 0, S)
 
         h2 = [keep.tile([P, 2 * S], F32, name="h2_%d" % t, align_bytes=64) for t in range(PACK)]
         sg = [keep.tile([P, 2 * S], F32, name="sg%d" % t, align_bytes=64) for t in range(PACK)]
-        other = [row_tile("other%d" % t) for t in range(PACK)]
-        difference = [row_tile("difference%d" % t) for t in range(PACK)]
+        other = {}
+        difference = {}
         result = [row_tile("result%d" % t) for t in range(PACK)]
         out_rows = out.rearrange("(p t) s -> p t s", t=PACK)
 
@@ -223,6 +231,7 @@ def tile_picked_codesendgedb_none_p_kernel(
                 )
 
         def duplicate(t, pieces):
+            other[t] = row_tile("other%d" % t, "other0")
             for a, b in pieces:
                 nc.vector.tensor_copy(other[t][:, a:b], sg[t][:, a:b])
 
@@ -230,7 +239,8 @@ def tile_picked_codesendgedb_none_p_kernel(
             nc.vector.scalar_tensor_tensor(result[t][:, a:b], difference[t][:, a:b], -1.5, h2[t][:, a:b], ALU.mult, ALU.mult)
             nc.sync.dma_start(out_rows[:, t, a:b], result[t][:, a:b])
 
-        nc.scalar.activation(h2[0][:, 0:S], h2_banks[0][:], ACT.Copy, scale=0.0625)
+        nc.vector.tensor_scalar(h2[0][:, HALF:S], h2_early[:], 0.0625, None, ALU.mult)
+        nc.scalar.activation(h2[0][:, 0:HALF], h2_late[:], ACT.Copy, scale=0.0625)
         leave_bank(1)
         leave_bank(2)
         fetch_sg(0, halves)
@@ -241,12 +251,16 @@ def tile_picked_codesendgedb_none_p_kernel(
         for t in range(2):
             if t > 0:
                 duplicate(t, [(0, S)])
-            for a, b in halves if t == 0 else [(0, S)]:
+            difference[t] = row_tile("difference%d" % t)
+            for a, b in halves:
                 nc.vector.tensor_tensor(
                     difference[t][:, a:b], sg[t][:].indirect(entries(n4_list, a, b)), other[t][:, a:b], ALU.subtract
                 )
-            finish(t, 0, S)
+            for a, b in halves:
+                finish(t, a, b)
         for t in range(2, PACK):
+            other[t] = row_tile("other%d" % t)
+            difference[t] = row_tile("difference%d" % t, "other0" if t == 2 else None)
             for a, b in halves:
                 nc.scalar.activation(other[t][:, a:b], sg[t][:].indirect(entries(n4_list, a, b)), ACT.Copy)
             for a, b in halves:

@@ -46,7 +46,7 @@ def tile_picked_codesendgedb_none_p_kernel(
 
         d_bytes = keep.tile([P, G], U8, name="d_bytes", align_bytes=64)
         x_bytes = keep.tile([P, T], U8, name="x_bytes", align_bytes=64)
-        planes = [keep.tile([P, width], U8, name="plane%d" % i, align_bytes=64) for i, width in enumerate((H + S, H))]
+        planes = [keep.tile([P, H], U8, name="plane%d" % i, align_bytes=64) for i in range(2)]
         nc.vector.memset(d_bytes[:].bitcast(I32), 0)
         nc.vector.memset(x_bytes[:].bitcast(I32), 0)
         for plane in planes:
@@ -55,13 +55,14 @@ def tile_picked_codesendgedb_none_p_kernel(
         k1_list = load_list("k1_list", k1)
         offs_list = load_list("offs_list", offs)
         nc.sync.dma_start(d_bytes[0:P:8, :].bitcast(I32), d_scales[0].bitcast(I32))
-        nc.sync.dma_start(x_bytes[0:P:8, :].bitcast(I32), x_scales[0].bitcast(I32))
+        for q in range(4):
+            nc.scalar.dma_start(x_bytes[32 * q : 32 * q + 4, :].bitcast(I32), x_scales[0, 4 * q : 4 * q + 4, :].bitcast(I32))
         x_table = keep.tile([P, T], I32, name="x_table", align_bytes=64)
         nc.sync.dma_start(x_table[:], x_words[0].rearrange("p c r -> p (c r)").bitcast(I32))
-        k2_list = load_list("k2_list", k2)
-        n2_list = load_list("n2_list", n2)
         d_table = keep.tile([P, G], I32, name="d_table", align_bytes=64)
         nc.sync.dma_start(d_table[:], d_words[0].rearrange("p c r -> p (c r)").bitcast(I32))
+        k2_list = load_list("k2_list", k2)
+        n2_list = load_list("n2_list", n2)
         n1_list = load_list("n1_list", n1)
         n3_list = load_list("n3_list", n3)
         n4_list = load_list("n4_list", n4)
@@ -69,7 +70,7 @@ def tile_picked_codesendgedb_none_p_kernel(
         slope = keep.tile([P, PACK], F32, name="slope")
         threshold = keep.tile([P, PACK], F32, name="threshold")
         for column, source in ((gain, gs), (slope, sl), (threshold, th)):
-            nc.scalar.dma_start(column[:], source.rearrange("(p t) o -> p (t o)", t=PACK))
+            nc.gpsimd.dma_start(column[:], source.rearrange("(p t) o -> p (t o)", t=PACK))
 
         product = keep.tile([P, PACK], F32, name="product")
         bias = keep.tile([P, PACK], F32, name="bias")
@@ -87,20 +88,19 @@ def tile_picked_codesendgedb_none_p_kernel(
 
         def deal_words(picked, dealt, start, stop):
             nc.vector.tensor_copy(
-                dealt[:].rearrange("p (t m) -> p m t", t=PACK)[:, start // PACK : stop // PACK, :],
-                picked[:].rearrange("p (m t) -> p m t", t=PACK),
+                dealt[:].rearrange("p (t c i) -> p c t i", t=PACK, i=4)[:, start // 16 : stop // 16, :, :],
+                picked[:].rearrange("p (c i t) -> p c t i", t=PACK, i=4),
             )
 
         picked_bytes1 = keep.tile([P, H], U8, name="picked_bytes1", align_bytes=64)
         nc.vector.tensor_copy(picked_bytes1[:], d_bytes[:].indirect(k1_list[:]))
-        xq_bytes = keep.tile([P, S], U8, name="xq_bytes", align_bytes=64)
-        nc.vector.tensor_copy(xq_bytes[:], x_bytes[:].indirect(offs_list[:]))
-        dealt_bytes1 = keep.tile([P, H + S], U8, name="dealt_bytes1", align_bytes=64)
+        dealt_bytes1 = keep.tile([P, H], U8, name="dealt_bytes1", align_bytes=64)
         deal_bytes(picked_bytes1, dealt_bytes1)
-        nc.vector.tensor_copy(dealt_bytes1[:, H:].bitcast(I32), xq_bytes[:].bitcast(I32))
-        place_bytes(dealt_bytes1, planes[0], [nc.sync, nc.scalar])
+        place_bytes(dealt_bytes1, planes[0], [nc.scalar])
         xq_words = keep.tile([P, S], U32, name="xq_words", align_bytes=64)
         nc.vector.tensor_copy(xq_words[:], x_table[:].bitcast(U32).indirect(offs_list[:]))
+        xq_bytes = keep.tile([P, S], U8, name="xq_bytes", tag="picked_bytes1", align_bytes=64)
+        nc.vector.tensor_copy(xq_bytes[:], x_bytes[:].indirect(offs_list[:]))
         w1 = keep.tile([P, H], U32, name="w1", align_bytes=64)
         picked1 = [keep.tile([P, HALF], U32, name="picked1_%d" % i, tag="picked%d" % i, align_bytes=64) for i in range(2)]
         for picked, (a, b) in zip(picked1, halves):
@@ -113,7 +113,7 @@ def tile_picked_codesendgedb_none_p_kernel(
             columns = slice(P * t, P * (t + 1))
             nc.tensor.matmul_mx(
                 h_banks[t][:], lhsT=w1[:, columns].bitcast(FP8X4), lhsT_scale=planes[0][:, columns],
-                rhs=xq_words[:].bitcast(FP8X4), rhs_scale=planes[0][:, H:], start=True, stop=True,
+                rhs=xq_words[:].bitcast(FP8X4), rhs_scale=xq_bytes[:], start=True, stop=True,
             )
 
         picked_bytes2 = keep.tile([P, H], U8, name="picked_bytes2", tag="picked0", align_bytes=64)

from contextlib import ExitStack

import concourse.mybir as mybir

K, T, S, G, H = 512, 1024, 512, 2048, 512
FLOPS = 2 * 2 * K * H * S

F32 = mybir.dt.float32
BF16 = mybir.dt.bfloat16
I32 = mybir.dt.int32
U32 = mybir.dt.uint32
U16 = mybir.dt.uint16
U8 = mybir.dt.uint8
FP8X4 = mybir.dt.float8_e4m3fn_x4
ALU = mybir.AluOpType
ACT = mybir.ActivationFunctionType

P = 128
PACK = 4
HALF = S // 2
SPLIT = 320
WIDE = 704
FIRST = 32


def entries(offsets, start, stop):
    return offsets[:, start // 16 : stop // 16]


def tile_picked_codesendgedb_none_p_kernel(
    tc, x_words, x_scales, d_words, d_scales, gs, sl, th, offs, k1, n1, n2, k2, n3, n4, out
):
    nc = tc.nc
    halves = [(0, HALF), (HALF, S)]
    with ExitStack() as ctx:
        keep = ctx.enter_context(tc.tile_pool(name="keep", bufs=1))
        psum = ctx.enter_context(tc.psum_pool(name="psum", bufs=1))

        def load_list(name, source):
            offsets = keep.tile([P, S // 16], U16, name=name)
            nc.sync.dma_start(offsets[:], source)
            return offsets

        def row_tile(name, tag=None):
            return keep.tile([P, S], F32, name=name, tag=tag or name, align_bytes=64)

        d_bytes = keep.tile([P, G], U8, name="d_bytes", align_bytes=64)
        x_bytes = keep.tile([P, T], U8, name="x_bytes", align_bytes=64)
        planes = [keep.tile([P, H], U8, name="plane%d" % i, align_bytes=64) for i in range(2)]
        nc.vector.memset(d_bytes[:].bitcast(I32), 0)
        nc.vector.memset(x_bytes[:].bitcast(I32), 0)
        for plane in planes:
            nc.vector.memset(plane[:].bitcast(I32), 0)

        k1_list = load_list("k1_list", k1)
        offs_list = load_list("offs_list", offs)
        nc.sync.dma_start(d_bytes[0:P:8, :].bitcast(I32), d_scales[0].bitcast(I32))
        for q in range(4):
            nc.scalar.dma_start(x_bytes[32 * q : 32 * q + 4, :].bitcast(I32), x_scales[0, 4 * q : 4 * q + 4, :].bitcast(I32))
        x_table = keep.tile([P, T], I32, name="x_table", align_bytes=64)
        nc.sync.dma_start(x_table[:], x_words[0].rearrange("p c r -> p (c r)").bitcast(I32))
        d_table = keep.tile([P, G], I32, name="d_table", align_bytes=64)
        nc.sync.dma_start(d_table[:], d_words[0].rearrange("p c r -> p (c r)").bitcast(I32))
        k2_list = load_list("k2_list", k2)
        n2_list = load_list("n2_list", n2)
        n1_list = load_list("n1_list", n1)
        n3_list = load_list("n3_list", n3)
        n4_list = load_list("n4_list", n4)
        gain = keep.tile([P, PACK], F32, name="gain")
        slope = keep.tile([P, PACK], F32, name="slope")
        threshold = keep.tile([P, PACK], F32, name="threshold")
        for column, source in ((gain, gs), (slope, sl), (threshold, th)):
            nc.gpsimd.dma_start(column[:], source.rearrange("(p t) o -> p (t o)", t=PACK))

        product = keep.tile([P, PACK], F32, name="product")
        bias = keep.tile([P, PACK], F32, name="bias")
        nc.gpsimd.tensor_tensor(product[:], slope[:], threshold[:], ALU.mult)
        nc.gpsimd.tensor_scalar(bias[:], product[:], -1.0, 0.0, ALU.mult, ALU.add)

        def deal_bytes(picked, dealt):
            nc.vector.tensor_copy(
                dealt[:, 0:H].rearrange("p (t m) -> p t m", t=PACK), picked[:].rearrange("p (m t) -> p t m", t=PACK)
            )

        def place_bytes(dealt, plane, queues):
            for q in range(4):
                queues[q % len(queues)].dma_start(plane[32 * q : 32 * q + 4, :].bitcast(I32), dealt[32 * q : 32 * q + 32 : 8, :].bitcast(I32))

        def deal_words(picked, dealt, start, stop):
            nc.vector.tensor_copy(
                dealt[:].rearrange("p (t c i) -> p c t i", t=PACK, i=4)[:, start // 16 : stop // 16, :, :],
                picked[:].rearrange("p (c i t) -> p c t i", t=PACK, i=4),
            )

        picked_bytes1 = keep.tile([P, H], U8, name="picked_bytes1", align_bytes=64)
        nc.vector.tensor_copy(picked_bytes1[:], d_bytes[:].indirect(k1_list[:]))
        dealt_bytes1 = keep.tile([P, H], U8, name="dealt_bytes1", align_bytes=64)
        deal_bytes(picked_bytes1, dealt_bytes1)
        place_bytes(dealt_bytes1, planes[0], [nc.scalar])
        xq_words = keep.tile([P, S], U32, name="xq_words", align_bytes=64)
        nc.vector.tensor_copy(xq_words[:], x_table[:].bitcast(U32).indirect(offs_list[:]))
        xq_bytes = keep.tile([P, S], U8, name="xq_bytes", tag="picked_bytes1", align_bytes=64)
        nc.vector.tensor_copy(xq_bytes[:], x_bytes[:].indirect(offs_list[:]))
        w1 = keep.tile([P, H], U32, name="w1", align_bytes=64)
        picked1 = [keep.tile([P, HALF], U32, name="picked1_%d" % i, tag="picked%d" % i, align_bytes=64) for i in range(2)]
        for picked, (a, b) in zip(picked1, halves):
            nc.vector.tensor_copy(picked[:], d_table[:].bitcast(U32).indirect(entries(k1_list, a, b)))
        for picked, (a, b) in zip(picked1, halves):
            deal_words(picked, w1, a, b)

        h_banks = [psum.tile([P, S], F32, name="h_bank%d" % t) for t in range(PACK)]
        for t in range(PACK):
            columns = slice(P * t, P * (t + 1))
            nc.tensor.matmul_mx(
                h_banks[t][:], lhsT=w1[:, columns].bitcast(FP8X4), lhsT_scale=planes[0][:, columns],
                rhs=xq_words[:].bitcast(FP8X4), rhs_scale=xq_bytes[:], start=True, stop=True,
            )

        picked_bytes2 = keep.tile([P, H], U8, name="picked_bytes2", tag="picked0", align_bytes=64)
        picked2 = keep.tile([P, H], U32, name="picked2", tag="picked1", align_bytes=64)
        w2 = keep.tile([P, H], U32, name="w2", align_bytes=64)
        nc.vector.tensor_copy(picked_bytes2[:], d_bytes[:].indirect(k2_list[:]))
        nc.vector.tensor_copy(picked2[:], d_table[:].bitcast(U32).indirect(k2_list[:]))
        dealt_bytes2 = keep.tile([P, H], U8, name="dealt_bytes2", align_bytes=64)
        deal_bytes(picked_bytes2, dealt_bytes2)
        place_bytes(dealt_bytes2, planes[1], [nc.sync])
        deal_words(picked2, w2, 0, H)

        gates = [row_tile("gate%d" % t) for t in range(PACK)]
        h = [keep.tile([P, WIDE], F32, name="h%d" % t, align_bytes=64) for t in range(PACK)]
        fetched = [row_tile("fetched%d" % t) for t in range(PACK)]
        larger = {}

        def gate(t, a, b):
            nc.scalar.activation(gates[t][:, a:b], h_banks[t][:, a:b], ACT.Sigmoid, scale=0.0625)

        def take_larger(t, tag=None):
            larger[t] = row_tile("larger%d" % t, tag)
            nc.vector.scalar_tensor_tensor(larger[t][:], h_banks[t][:], 0.0625, fetched[t][:], ALU.mult, ALU.max)

        def send(engine, window, t, a, b):
            target = window[:].indirect(entries(n1_list, a, b))
            if engine == "vector":
                nc.vector.tensor_copy(target, larger[t][:, a:b])
            else:
                nc.scalar.activation(target, larger[t][:, a:b], ACT.Copy)

        z_rows = keep.tile([P, PACK, S], BF16, name="z_rows", align_bytes=64)

        def weigh(t, window, a, b):
            nc.vector.scalar_tensor_tensor(z_rows[:, t, a:b], window[:, a:b], gain[:, t : t + 1], gates[t][:, a:b], ALU.mult, ALU.mult)

        gate(0, 0, FIRST)
        for t in range(PACK):
            nc.scalar.activation(h[t][:, 0:S], h_banks[t][:], ACT.Copy, scale=0.0625)
            nc.scalar.activation(fetched[t][:], h[t][:].indirect(n2_list[:]), ACT.Copy)

        take_larger(0)
        sent0 = keep.tile([P, WIDE], F32, name="sent0", align_bytes=64)
        send("vector", sent0, 0, 0, S)
        take_larger(1, "larger0")
        take_larger(2)
        take_larger(3)
        sent3 = keep.tile([P, WIDE], F32, name="sent3", align_bytes=64)
        send("vector", sent3, 3, 0, S)
        sent1 = row_tile("sent1", tag="h3")
        send("scalar", sent1, 1, 0, HALF)
        sent2 = row_tile("sent2", tag="fetched3")
        send("scalar", sent2, 2, 0, SPLIT)
        send("vector", sent2, 2, SPLIT, S)
        for t in (0, 3, 2, 1):
            gate(t, FIRST if t == 0 else 0, S)
        send("scalar", sent1, 1, HALF, S)
        weigh(0, sent0, 0, S)
        weigh(3, sent3, 0, S)
        weigh(2, sent2, 0, S)

        z_grouped = keep.tile([P, S, PACK], BF16, name="z_grouped", align_bytes=64)
        z_words = keep.tile([P, S], U32, name="z_words", align_bytes=64)
        z_bytes = keep.tile([P, S], U8, name="z_bytes", align_bytes=64)

        def group(copy, a, b):
            copy(
                z_grouped[:, a:b, :].rearrange("p (c i) t -> p c t i", i=4),
                z_rows[:, :, a:b].rearrange("p t (c i) -> p c t i", i=4),
            )

        def quantise(a, b):
            nc.vector.quantize_mx(z_words[:, a:b].bitcast(FP8X4), z_bytes[:, a:b], z_grouped[:, a:b, :].rearrange("p s t -> p (s t)"))

        weigh(1, sent1, 0, P)
        weigh(1, sent1, HALF, S)
        weigh(1, sent1, P, HALF)
        group(nc.scalar.copy, 0, P)
        group(nc.vector.tensor_copy, HALF, S)
        group(nc.vector.tensor_copy, P, HALF)
        quantise(HALF, S)
        quantise(0, HALF)

        def second_product(bank, t, a, b):
            columns = slice(P * t, P * (t + 1))
            nc.tensor.matmul_mx(
                bank[:], lhsT=w2[:, columns].bitcast(FP8X4), lhsT_scale=planes[1][:, columns],
                rhs=z_words[:, a:b].bitcast(FP8X4), rhs_scale=z_bytes[:, a:b], start=True, stop=True,
            )

        h2_late = psum.tile([P, HALF], F32, name="h2_late")
        h2_early = psum.tile([P, HALF], F32, name="h2_early", tag="h_bank0")
        second_product(h2_early, 0, HALF, S)
        second_product(h2_late, 0, 0, HALF)
        h2_banks = {}
        for t in range(1, PACK):
            h2_banks[t] = psum.tile([P, S], F32, name="h2_bank%d" % t)
            second_product(h2_banks[t], t, 0, S)

        h2 = [keep.tile([P, 2 * S], F32, name="h2_%d" % t, align_bytes=64) for t in range(PACK)]
        sg = [keep.tile([P, 2 * S], F32, name="sg%d" % t, align_bytes=64) for t in range(PACK)]
        other = {}
        difference = {}
        result = [row_tile("result%d" % t) for t in range(PACK)]
        out_rows = out.rearrange("(p t) s -> p t s", t=PACK)

        def leave_bank(t):
            nc.vector.tensor_scalar(h2[t][:, 0:S], h2_banks[t][:], 0.0625, None, ALU.mult)

        def fetch_sg(t, pieces):
            for a, b in pieces:
                nc.scalar.activation(
                    sg[t][:, a:b], h2[t][:].indirect(entries(n3_list, a, b)), ACT.Sigmoid,
                    bias=bias[:, t : t + 1], scale=slope[:, t : t + 1],
                )

        def duplicate(t, pieces):
            other[t] = row_tile("other%d" % t, "other0")
            for a, b in pieces:
                nc.vector.tensor_copy(other[t][:, a:b], sg[t][:, a:b])

        def finish(t, a, b):
            nc.vector.scalar_tensor_tensor(result[t][:, a:b], difference[t][:, a:b], -1.5, h2[t][:, a:b], ALU.mult, ALU.mult)
            nc.sync.dma_start(out_rows[:, t, a:b], result[t][:, a:b])

        nc.vector.tensor_scalar(h2[0][:, HALF:S], h2_early[:], 0.0625, None, ALU.mult)
        nc.scalar.activation(h2[0][:, 0:HALF], h2_late[:], ACT.Copy, scale=0.0625)
        leave_bank(1)
        leave_bank(2)
        fetch_sg(0, halves)
        duplicate(0, halves)
        leave_bank(3)
        for t in range(1, PACK):
            fetch_sg(t, [(0, S)])
        for t in range(2):
            if t > 0:
                duplicate(t, [(0, S)])
            difference[t] = row_tile("difference%d" % t)
            for a, b in halves:
                nc.vector.tensor_tensor(
                    difference[t][:, a:b], sg[t][:].indirect(entries(n4_list, a, b)), other[t][:, a:b], ALU.subtract
                )
            for a, b in halves:
                finish(t, a, b)
        for t in range(2, PACK):
            other[t] = row_tile("other%d" % t)
            difference[t] = row_tile("difference%d" % t, "other0" if t == 2 else None)
            for a, b in halves:
                nc.scalar.activation(other[t][:, a:b], sg[t][:].indirect(entries(n4_list, a, b)), ACT.Copy)
            for a, b in halves:
                nc.vector.tensor_tensor(difference[t][:, a:b], other[t][:, a:b], sg[t][:, a:b], ALU.subtract)
            for a, b in halves:
                finish(t, a, b)
